import numpy as np
import ml_dtypes


def mxq(x, axis, fmt="e4m3"):
    dtype, down = {"e4m3": (ml_dtypes.float8_e4m3fn, 7), "e5m2": (ml_dtypes.float8_e5m2, 14)}[fmt]
    v = np.moveaxis(np.asarray(x, np.float32).astype(ml_dtypes.bfloat16).astype(np.float64), axis, -1)
    blocks = v.reshape(v.shape[:-1] + (-1, 32))
    amax = np.abs(blocks).max(-1, keepdims=True)
    byte = np.maximum(np.where(amax > 0, np.frexp(amax)[1] - 1 + 127, 0) - down, 1)
    scale = np.exp2(byte - 127.0)
    codes = (blocks / scale).astype(np.float32).astype(dtype).astype(np.float64)
    return np.moveaxis((codes * scale).reshape(v.shape), -1, axis)


WIDE = False


def mx_kscale(k):
    if not WIDE:
        return np.ones(k)
    levels = np.array([30, -30])
    if k % 512:
        return np.exp2(np.random.permutation(np.resize(levels, k // 32))).repeat(32)
    a = np.empty((k // 512, 16))
    for p in range(k // 512):
        a[p, :8] = np.random.permutation(np.resize(levels, 8))
        for g in range(8):
            far = levels[np.abs(levels - a[p, g]) >= 10]
            a[p, g + 8] = far[np.random.randint(len(far))]
    return np.exp2(a.ravel()).repeat(32)


def f64(x):
    return np.asarray(x).astype(np.float64)


E2M1 = np.array([0.0, 0.5, 1.0, 1.5, 2.0, 3.0, 4.0, 6.0, -0.0, -0.5, -1.0, -1.5, -2.0, -3.0, -4.0, -6.0])


def pack_weight(w, fmt):
    k, n = w.shape
    w = f64(np.asarray(w, np.float32).astype(ml_dtypes.bfloat16)).reshape(k // 32, 32, n)
    amax = np.abs(w).max(1)
    if fmt == "e4m3":
        byte = np.frexp(amax)[1] - 1 + 127 - 7
    else:
        mant, ex = np.frexp(amax / 6.0)
        byte = np.where(mant > 0.5, ex, ex - 1) + 127
    byte = np.clip(np.where(amax > 0, byte, 1), 1, 254)
    scaled = (w * np.exp2(127.0 - byte)[:, None, :]).reshape(k, n).astype(np.float32)
    by_word = np.ascontiguousarray(scaled.reshape(k // 512, 128, 4, n).transpose(0, 1, 3, 2))
    if fmt == "e4m3":
        words = by_word.astype(ml_dtypes.float8_e4m3fn).view(np.uint8)
    else:
        c = by_word.astype(ml_dtypes.float4_e2m1fn).view(np.uint8) & 0xF
        words = (c[..., 0::2] | (c[..., 1::2] << 4)).reshape(k // 512, 128, 2 * n)
    return np.ascontiguousarray(words), np.ascontiguousarray(byte.astype(np.uint8).reshape(k // 512, 16, n))


def unpack_weight(words, scales, fmt):
    g, _, n = scales.shape
    words = np.ascontiguousarray(words).reshape(g, 128, n, -1)
    if fmt == "e4m3":
        vals = words.view(ml_dtypes.float8_e4m3fn).astype(np.float64)
    else:
        nib = np.empty((g, 128, n, 4), np.uint8)
        nib[..., 0::2] = words & 0xF
        nib[..., 1::2] = words >> 4
        vals = E2M1[nib]
    vals = vals * np.repeat(np.exp2(scales.astype(np.float64) - 127.0), 8, axis=1)[..., None]
    return vals.transpose(0, 1, 3, 2).reshape(g * 512, n)


H, D, T = 1536, 512, 512


def setup_inputs():
    n = np.random.standard_normal
    s = mx_kscale(H)[:, None]
    p_wg = pack_weight(n((H, D)) / np.sqrt(H) / s, "e2m1")
    p_wu = pack_weight(n((H, D)) / np.sqrt(H) / s, "e4m3")
    return {
        "g": n((H, T)).astype(np.float32),
        "u": n((H, T)).astype(np.float32),
        "dh": (np.exp(0.5 * n((1, T))) * n((H, T)) * s).astype(np.float32),
        "wg_words": p_wg[0],
        "wg_scales": p_wg[1],
        "wu_words": p_wu[0],
        "wu_scales": p_wu[1],
    }


def reference(g, u, dh, wg_words, wg_scales, wu_words, wu_scales):
    sg = 1.0 / (1.0 + np.exp(-f64(g)))
    dg_ = mxq(f64(dh) * f64(u) * sg * (1.0 + f64(g) * (1.0 - sg)), 0, "e5m2")
    du_ = mxq(f64(dh) * f64(g) * sg, 0, "e5m2")
    wg_ = unpack_weight(wg_words, wg_scales, "e2m1")
    wu_ = unpack_weight(wu_words, wu_scales, "e4m3")
    y = wg_.T @ dg_ + wu_.T @ du_
    return y

@@ -1,0 +1,221 @@
+from contextlib import ExitStack
+
+import concourse.mybir as mybir
+
+H, D, T = 1536, 512, 512
+FLOPS = 2 * 2 * H * D * T
+
+F32 = mybir.dt.float32
+BF16 = mybir.dt.bfloat16
+I32 = mybir.dt.int32
+U32 = mybir.dt.uint32
+U8 = mybir.dt.uint8
+E5M2X4 = mybir.dt.float8_e5m2_x4
+E4M3X4 = mybir.dt.float8_e4m3fn_x4
+E2M1X4 = mybir.dt.float4_e2m1fn_x4
+ACT = mybir.ActivationFunctionType
+ALU = mybir.AluOpType
+
+P = 128
+PACK = 4
+PASSES = H // (P * PACK)
+M_TILES = D // P
+
+
+def tile_mix_glubwd_fm_none_kernel(tc, g, u, dh, wg_words, wg_scales, wu_words, wu_scales, out):
+    nc = tc.nc
+    with ExitStack() as ctx:
+        keep = ctx.enter_context(tc.tile_pool(name="keep", bufs=1))
+        work = ctx.enter_context(tc.tile_pool(name="work", bufs=2))
+        psum = ctx.enter_context(tc.psum_pool(name="psum", bufs=1))
+        ctx.enter_context(tc.manual_schedule())
+
+        def per_pass(name, shape, dtype):
+            return [keep.tile(shape, dtype, name=name + str(a), align_bytes=64) for a in range(PASSES)]
+
+        g_sb = per_pass("g_sb", [P, PACK, T], F32)
+        u_sb = per_pass("u_sb", [P, PACK, T], F32)
+        dh_sb = per_pass("dh_sb", [P, PACK, T], F32)
+        neg_a = per_pass("neg_a", [P, PACK, T], F32)
+        du_bf = per_pass("du_bf", [P, T, PACK], BF16)
+        dg_bf = per_pass("dg_bf", [P, T, PACK], BF16)
+        du_codes = per_pass("du_codes", [P, T], U32)
+        dg_codes = per_pass("dg_codes", [P, T], U32)
+        du_scale = per_pass("du_scale", [P, T], U8)
+        dg_scale = per_pass("dg_scale", [P, T], U8)
+        wg_sb = keep.tile([P, PASSES, 2 * D], U8, align_bytes=64)
+        wu_sb = keep.tile([P, PASSES, 4 * D], U8, align_bytes=64)
+        wg_plane = keep.tile([P, PASSES, D], U8, align_bytes=64)
+        wu_plane = keep.tile([P, PASSES, D], U8, align_bytes=64)
+        warm = keep.tile([P, 8], F32, align_bytes=64)
+        warm_out = keep.tile([P, 8], F32, align_bytes=64)
+        acc = [psum.tile([P, T], F32, name="acc" + str(m)) for m in range(M_TILES)]
+        res = [keep.tile([P, T], F32, name="res" + str(m), align_bytes=64) for m in range(M_TILES)]
+
+        scratch = {}
+
+        def stage(kind, a):
+            if (kind, a) not in scratch:
+                scratch[(kind, a)] = work.tile([P, PACK, T], F32, name=kind, align_bytes=64)
+            return scratch[(kind, a)]
+
+        nc.vector.memset(warm[:], 0.0)
+        nc.scalar.activation(out=warm_out[:], in_=warm[:], func=ACT.Sigmoid)
+        nc.vector.memset(wg_plane[:].bitcast(U32), 0)
+        nc.vector.memset(wu_plane[:].bitcast(U32), 0)
+
+        all_t = slice(0, T)
+        all_j = slice(0, PACK)
+        lo_j, hi_j = slice(0, 2), slice(2, 4)
+        lo_t, hi_t = slice(0, T // 2), slice(T // 2, T)
+
+        def load(dst, src, a, js, ts):
+            rows = src[a * P * PACK:(a + 1) * P * PACK, :].rearrange("(p j) t -> p j t", j=PACK)
+            nc.sync.dma_start(out=dst[a][:, js, ts], in_=rows[:, js, ts])
+
+        head = [(slice(0, 1), lo_t), (slice(0, 1), hi_t), (slice(1, 2), all_t), (slice(2, 3), all_t), (slice(3, 4), all_t)]
+        for js, ts in head[:3]:
+            load(g_sb, g, 0, js, ts)
+            load(dh_sb, dh, 0, js, ts)
+        for js, ts in head[3:]:
+            load(g_sb, g, 0, js, ts)
+        for js, ts in head[3:]:
+            load(dh_sb, dh, 0, js, ts)
+        for dst, src, a in ((u_sb, u, 0), (g_sb, g, 1), (u_sb, u, 1), (dh_sb, dh, 1)):
+            load(dst, src, a, lo_j, all_t)
+            load(dst, src, a, hi_j, all_t)
+        load(g_sb, g, 2, all_j, all_t)
+        load(dh_sb, dh, 2, all_j, all_t)
+        for plane, scales in ((wu_plane, wu_scales), (wg_plane, wg_scales)):
+            for q in range(4):
+                nc.sync.dma_start(
+                    out=plane[32 * q:32 * q + 4, :, :].bitcast(I32),
+                    in_=scales.bitcast(I32)[:, 4 * q:4 * q + 4, :].rearrange("a r n -> r a n"),
+                )
+        nc.sync.dma_start(out=wu_sb[:].bitcast(I32), in_=wu_words.rearrange("a p n i -> p a (n i)").bitcast(I32))
+        nc.sync.dma_start(out=wg_sb[:].bitcast(I32), in_=wg_words.rearrange("a p n -> p a n").bitcast(I32))
+        load(u_sb, u, 2, all_j, all_t)
+
+        def sigmoid(a, js, ts):
+            nc.scalar.activation(out=stage("sig", a)[:, js, ts], in_=g_sb[a][:, js, ts], func=ACT.Sigmoid)
+
+        def silu_neg(a, js, ts):
+            nc.scalar.activation(out=stage("siln", a)[:, js, ts], in_=g_sb[a][:, js, ts], func=ACT.Silu, scale=-1.0)
+
+        def make_a(a, js, ts):
+            nc.vector.scalar_tensor_tensor(
+                out=neg_a[a][:, js, ts], in0=stage("sig", a)[:, js, ts], scalar=-1.0, in1=dh_sb[a][:, js, ts],
+                op0=ALU.mult, op1=ALU.mult)
+
+        def make_du(a, js, ts):
+            nc.vector.tensor_tensor(
+                out=stage("neg_du", a)[:, js, ts], in0=neg_a[a][:, js, ts], in1=g_sb[a][:, js, ts], op=ALU.mult)
+
+        def make_q(a, js, ts):
+            nc.vector.scalar_tensor_tensor(
+                out=stage("neg_q", a)[:, js, ts], in0=stage("siln", a)[:, js, ts], scalar=-1.0, in1=u_sb[a][:, js, ts],
+                op0=ALU.add, op1=ALU.mult)
+
+        def rows_view(tile, ts):
+            return tile[:, :, ts].rearrange("p j (c i) -> p c j i", i=4)
+
+        def words_view(tile, ts):
+            return tile[:, ts, :].rearrange("p (c i) j -> p c j i", i=4)
+
+        def make_dg(a, ts):
+            nc.vector.tensor_tensor(
+                out=words_view(dg_bf[a], ts), in0=rows_view(neg_a[a], ts), in1=rows_view(stage("neg_q", a), ts), op=ALU.mult)
+
+        def round_du(a, ts):
+            nc.scalar.activation(out=words_view(du_bf[a], ts), in_=rows_view(stage("neg_du", a), ts), func=ACT.Copy, scale=-1.0)
+
+        def quantize(vals, codes, scale, ts):
+            nc.vector.quantize_mx(
+                out=codes[:, ts].bitcast(E5M2X4), scales=scale[:, ts], in_=vals[:, ts, :].rearrange("p t j -> p (t j)"))
+
+        def quant_du(a, ts):
+            quantize(du_bf[a], du_codes[a], du_scale[a], ts)
+
+        def quant_dg(a, ts):
+            quantize(dg_bf[a], dg_codes[a], dg_scale[a], ts)
+
+        def mm_du(a, m, start):
+            nc.tensor.matmul_mx(
+                out=acc[m][:], lhsT=wu_sb[:, a, 4 * P * m:4 * P * (m + 1)].bitcast(E4M3X4),
+                lhsT_scale=wu_plane[:, a, P * m:P * (m + 1)],
+                rhs=du_codes[a][:].bitcast(E5M2X4), rhs_scale=du_scale[a][:], start=start, stop=False)
+
+        def mm_dg(a, m, stop):
+            nc.tensor.matmul_mx(
+                out=acc[m][:], lhsT=wg_sb[:, a, 2 * P * m:2 * P * (m + 1)].bitcast(E2M1X4),
+                lhsT_scale=wg_plane[:, a, P * m:P * (m + 1)],
+                rhs=dg_codes[a][:].bitcast(E5M2X4), rhs_scale=dg_scale[a][:], start=False, stop=stop)
+
+        def q_three(a):
+            make_q(a, lo_j, all_t)
+            make_q(a, hi_j, lo_t)
+            make_q(a, hi_j, hi_t)
+
+        for js, ts in head:
+            sigmoid(0, js, ts)
+        for n in range(len(head) + 1):
+            if n < len(head):
+                make_a(0, *head[n])
+            if n > 0:
+                make_du(0, *head[n - 1])
+        silu_neg(0, slice(0, 1), all_t)
+        silu_neg(0, slice(1, 2), all_t)
+        silu_neg(0, hi_j, all_t)
+        silu_neg(1, lo_j, all_t)
+        silu_neg(1, hi_j, all_t)
+        make_q(0, slice(0, 1), all_t)
+        make_q(0, slice(1, 2), all_t)
+        make_q(0, hi_j, lo_t)
+        make_q(0, hi_j, hi_t)
+        make_dg(0, lo_t)
+        make_dg(0, hi_t)
+        make_q(1, lo_j, all_t)
+        quant_dg(0, all_t)
+        make_q(1, hi_j, all_t)
+        sigmoid(1, lo_j, all_t)
+        sigmoid(1, hi_j, all_t)
+        round_du(0, all_t)
+        sigmoid(2, all_j, all_t)
+        make_a(1, lo_j, all_t)
+        make_a(1, hi_j, all_t)
+        make_du(1, lo_j, all_t)
+        make_du(1, hi_j, all_t)
+        round_du(1, all_t)
+        make_dg(1, all_t)
+        quant_du(0, all_t)
+        make_a(2, lo_j, all_t)
+        quant_dg(1, all_t)
+        make_a(2, hi_j, all_t)
+        make_du(2, lo_j, all_t)
+        make_du(2, hi_j, all_t)
+        silu_neg(2, lo_j, all_t)
+        silu_neg(2, hi_j, all_t)
+        round_du(2, all_t)
+        quant_du(1, all_t)
+        q_three(2)
+        make_dg(2, lo_t)
+        quant_du(2, all_t)
+        make_dg(2, hi_t)
+        quant_dg(2, lo_t)
+        quant_dg(2, hi_t)
+
+        for m in range(M_TILES):
+            mm_du(0, m, True)
+        for a in range(PASSES - 1):
+            for m in range(M_TILES):
+                mm_dg(a, m, False)
+        for a in range(1, PASSES):
+            for m in range(M_TILES):
+                mm_du(a, m, False)
+        for m in range(M_TILES):
+            mm_dg(PASSES - 1, m, True)
+            if m % 2 == 0:
+                nc.vector.tensor_copy(out=res[m][:], in_=acc[m][:])
+            else:
+                nc.scalar.copy(out=res[m][:], in_=acc[m][:])
+            nc.sync.dma_start(out=out[P * m:P * (m + 1), :], in_=res[m][:])

@@ -20,6 +20,9 @@ P = 128
 PACK = 4
 PASSES = H // (P * PACK)
 M_TILES = D // P
+LAST = PASSES - 1
+LATE = 256
+EARLY = T - LATE
 
 
 def tile_mix_glubwd_fm_none_kernel(tc, g, u, dh, wg_words, wg_scales, wu_words, wu_scales, out):
@@ -40,9 +43,9 @@ def tile_mix_glubwd_fm_none_kernel(tc, g, u, dh, wg_words, wg_scales, wu_words, 
         du_bf = per_pass("du_bf", [P, T, PACK], BF16)
         dg_bf = per_pass("dg_bf", [P, T, PACK], BF16)
         du_codes = per_pass("du_codes", [P, T], U32)
-        dg_codes = per_pass("dg_codes", [P, T], U32)
+        dg_codes = per_pass("dg_codes", [P, T + LATE], U32)
         du_scale = per_pass("du_scale", [P, T], U8)
-        dg_scale = per_pass("dg_scale", [P, T], U8)
+        dg_scale = per_pass("dg_scale", [P, T + LATE], U8)
         wg_sb = keep.tile([P, PASSES, 2 * D], U8, align_bytes=64)
         wu_sb = keep.tile([P, PASSES, 4 * D], U8, align_bytes=64)
         wg_plane = keep.tile([P, PASSES, D], U8, align_bytes=64)
@@ -50,6 +53,8 @@ def tile_mix_glubwd_fm_none_kernel(tc, g, u, dh, wg_words, wg_scales, wu_words, 
         warm = keep.tile([P, 8], F32, align_bytes=64)
         warm_out = keep.tile([P, 8], F32, align_bytes=64)
         acc = [psum.tile([P, T], F32, name="acc" + str(m)) for m in range(M_TILES)]
+        acc_late = [psum.tile([P, T], F32, name="acc_late" + str(m)) for m in range(M_TILES)]
+        part = [keep.tile([P, LATE], F32, name="part" + str(m), align_bytes=64) for m in range(M_TILES)]
         res = [keep.tile([P, T], F32, name="res" + str(m), align_bytes=64) for m in range(M_TILES)]
 
         scratch = {}
@@ -63,6 +68,8 @@ def tile_mix_glubwd_fm_none_kernel(tc, g, u, dh, wg_words, wg_scales, wu_words, 
         nc.scalar.activation(out=warm_out[:], in_=warm[:], func=ACT.Sigmoid)
         nc.vector.memset(wg_plane[:].bitcast(U32), 0)
         nc.vector.memset(wu_plane[:].bitcast(U32), 0)
+        nc.vector.memset(dg_codes[LAST][:, EARLY:T], 0)
+        nc.vector.memset(dg_scale[LAST][:, EARLY:T].bitcast(U32), 0)
 
         all_t = slice(0, T)
         all_j = slice(0, PACK)
@@ -85,15 +92,16 @@ def tile_mix_glubwd_fm_none_kernel(tc, g, u, dh, wg_words, wg_scales, wu_words, 
             load(dst, src, a, lo_j, all_t)
             load(dst, src, a, hi_j, all_t)
         load(g_sb, g, 2, all_j, all_t)
-        load(dh_sb, dh, 2, all_j, all_t)
-        for plane, scales in ((wu_plane, wu_scales), (wg_plane, wg_scales)):
+        load(dh_sb, dh, 2, lo_j, all_t)
+        load(dh_sb, dh, 2, hi_j, all_t)
+        for plane, scales in ((wg_plane, wg_scales), (wu_plane, wu_scales)):
             for q in range(4):
                 nc.sync.dma_start(
                     out=plane[32 * q:32 * q + 4, :, :].bitcast(I32),
                     in_=scales.bitcast(I32)[:, 4 * q:4 * q + 4, :].rearrange("a r n -> r a n"),
                 )
-        nc.sync.dma_start(out=wu_sb[:].bitcast(I32), in_=wu_words.rearrange("a p n i -> p a (n i)").bitcast(I32))
         nc.sync.dma_start(out=wg_sb[:].bitcast(I32), in_=wg_words.rearrange("a p n -> p a n").bitcast(I32))
+        nc.sync.dma_start(out=wu_sb[:].bitcast(I32), in_=wu_words.rearrange("a p n i -> p a (n i)").bitcast(I32))
         load(u_sb, u, 2, all_j, all_t)
 
         def sigmoid(a, js, ts):
@@ -129,43 +137,42 @@ def tile_mix_glubwd_fm_none_kernel(tc, g, u, dh, wg_words, wg_scales, wu_words, 
         def round_du(a, ts):
             nc.scalar.activation(out=words_view(du_bf[a], ts), in_=rows_view(stage("neg_du", a), ts), func=ACT.Copy, scale=-1.0)
 
-        def quantize(vals, codes, scale, ts):
+        def quantize(vals, codes, scale, ts, shift):
+            cols = slice(ts.start + shift, ts.stop + shift)
             nc.vector.quantize_mx(
-                out=codes[:, ts].bitcast(E5M2X4), scales=scale[:, ts], in_=vals[:, ts, :].rearrange("p t j -> p (t j)"))
+                out=codes[:, cols].bitcast(E5M2X4), scales=scale[:, cols], in_=vals[:, ts, :].rearrange("p t j -> p (t j)"))
 
         def quant_du(a, ts):
-            quantize(du_bf[a], du_codes[a], du_scale[a], ts)
+            quantize(du_bf[a], du_codes[a], du_scale[a], ts, 0)
 
-        def quant_dg(a, ts):
-            quantize(dg_bf[a], dg_codes[a], dg_scale[a], ts)
+        def quant_dg(a, ts, shift=0):
+            quantize(dg_bf[a], dg_codes[a], dg_scale[a], ts, shift)
 
-        def mm_du(a, m, start):
+        def mm_du(a, m):
             nc.tensor.matmul_mx(
                 out=acc[m][:], lhsT=wu_sb[:, a, 4 * P * m:4 * P * (m + 1)].bitcast(E4M3X4),
                 lhsT_scale=wu_plane[:, a, P * m:P * (m + 1)],
-                rhs=du_codes[a][:].bitcast(E5M2X4), rhs_scale=du_scale[a][:], start=start, stop=False)
+                rhs=du_codes[a][:].bitcast(E5M2X4), rhs_scale=du_scale[a][:], start=False, stop=False)
 
-        def mm_dg(a, m, stop):
+        def mm_dg(a, m, bank, cols, start, stop):
             nc.tensor.matmul_mx(
-                out=acc[m][:], lhsT=wg_sb[:, a, 2 * P * m:2 * P * (m + 1)].bitcast(E2M1X4),
+                out=bank[:], lhsT=wg_sb[:, a, 2 * P * m:2 * P * (m + 1)].bitcast(E2M1X4),
                 lhsT_scale=wg_plane[:, a, P * m:P * (m + 1)],
-                rhs=dg_codes[a][:].bitcast(E5M2X4), rhs_scale=dg_scale[a][:], start=False, stop=stop)
-
-        def q_three(a):
-            make_q(a, lo_j, all_t)
-            make_q(a, hi_j, lo_t)
-            make_q(a, hi_j, hi_t)
+                rhs=dg_codes[a][:, cols].bitcast(E5M2X4), rhs_scale=dg_scale[a][:, cols], start=start, stop=stop)
 
         for js, ts in head:
             sigmoid(0, js, ts)
-        for n in range(len(head) + 1):
-            if n < len(head):
-                make_a(0, *head[n])
-            if n > 0:
-                make_du(0, *head[n - 1])
+        for js, ts in head[:3]:
+            make_a(0, js, ts)
+            make_du(0, js, ts)
+        for js, ts in head[3:]:
+            make_a(0, js, ts)
+        for js, ts in head[3:]:
+            make_du(0, js, ts)
         silu_neg(0, slice(0, 1), all_t)
         silu_neg(0, slice(1, 2), all_t)
-        silu_neg(0, hi_j, all_t)
+        silu_neg(0, hi_j, lo_t)
+        silu_neg(0, hi_j, hi_t)
         silu_neg(1, lo_j, all_t)
         silu_neg(1, hi_j, all_t)
         make_q(0, slice(0, 1), all_t)
@@ -180,42 +187,55 @@ def tile_mix_glubwd_fm_none_kernel(tc, g, u, dh, wg_words, wg_scales, wu_words, 
         sigmoid(1, lo_j, all_t)
         sigmoid(1, hi_j, all_t)
         round_du(0, all_t)
-        sigmoid(2, all_j, all_t)
+        sigmoid(2, lo_j, all_t)
+        sigmoid(2, hi_j, all_t)
         make_a(1, lo_j, all_t)
         make_a(1, hi_j, all_t)
         make_du(1, lo_j, all_t)
         make_du(1, hi_j, all_t)
         round_du(1, all_t)
-        make_dg(1, all_t)
         quant_du(0, all_t)
         make_a(2, lo_j, all_t)
-        quant_dg(1, all_t)
         make_a(2, hi_j, all_t)
         make_du(2, lo_j, all_t)
         make_du(2, hi_j, all_t)
-        silu_neg(2, lo_j, all_t)
-        silu_neg(2, hi_j, all_t)
-        round_du(2, all_t)
         quant_du(1, all_t)
-        q_three(2)
-        make_dg(2, lo_t)
+        make_dg(1, all_t)
+        early = slice(0, EARLY)
+        late = slice(EARLY, T)
+        late_a = slice(EARLY, EARLY + LATE // 2)
+        late_b = slice(EARLY + LATE // 2, T)
+        silu_neg(2, all_j, early)
+        silu_neg(2, all_j, late)
+        round_du(2, all_t)
+        make_q(2, all_j, early)
+        quant_dg(1, all_t)
+        make_dg(2, early)
         quant_du(2, all_t)
-        make_dg(2, hi_t)
-        quant_dg(2, lo_t)
-        quant_dg(2, hi_t)
+        make_q(2, all_j, late_a)
+        quant_dg(2, early)
+        make_q(2, all_j, late_b)
+        make_dg(2, late_a)
+        make_dg(2, late_b)
+        quant_dg(2, late_a, LATE)
+        quant_dg(2, late_b, LATE)
 
         for m in range(M_TILES):
-            mm_du(0, m, True)
-        for a in range(PASSES - 1):
+            mm_dg(0, m, acc[m], all_t, True, False)
+        for a in range(2):
             for m in range(M_TILES):
-                mm_dg(a, m, False)
-        for a in range(1, PASSES):
-            for m in range(M_TILES):
-                mm_du(a, m, False)
+                mm_du(a, m)
         for m in range(M_TILES):
-            mm_dg(PASSES - 1, m, True)
-            if m % 2 == 0:
-                nc.vector.tensor_copy(out=res[m][:], in_=acc[m][:])
-            else:
-                nc.scalar.copy(out=res[m][:], in_=acc[m][:])
-            nc.sync.dma_start(out=out[P * m:P * (m + 1), :], in_=res[m][:])
+            mm_dg(1, m, acc[m], all_t, False, False)
+        for m in range(M_TILES):
+            mm_du(LAST, m)
+        for m in range(M_TILES):
+            mm_dg(LAST, m, acc[m], all_t, False, True)
+            nc.scalar.copy(out=res[m][:, early], in_=acc[m][:, early])
+            nc.sync.dma_start(out=out[P * m:P * (m + 1), early], in_=res[m][:, early])
+        for m in range(M_TILES):
+            nc.scalar.copy(out=part[m][:], in_=acc[m][:, late])
+        for m in range(M_TILES):
+            mm_dg(LAST, m, acc_late[m], slice(LATE, T + LATE), True, True)
+            nc.vector.tensor_tensor(out=res[m][:, late], in0=acc_late[m][:, late], in1=part[m][:], op=ALU.add)
+            nc.sync.dma_start(out=out[P * m:P * (m + 1), late], in_=res[m][:, late])

@@ -80,14 +80,14 @@ def tile_mix_glubwd_fm_none_kernel(tc, g, u, dh, wg_words, wg_scales, wu_words, 
             rows = src[a * P * PACK:(a + 1) * P * PACK, :].rearrange("(p j) t -> p j t", j=PACK)
             nc.sync.dma_start(out=dst[a][:, js, ts], in_=rows[:, js, ts])
 
-        head = [(slice(0, 1), lo_t), (slice(0, 1), hi_t), (slice(1, 2), all_t), (slice(2, 3), all_t), (slice(3, 4), all_t)]
-        for js, ts in head[:3]:
-            load(g_sb, g, 0, js, ts)
-            load(dh_sb, dh, 0, js, ts)
-        for js, ts in head[3:]:
-            load(g_sb, g, 0, js, ts)
-        for js, ts in head[3:]:
-            load(dh_sb, dh, 0, js, ts)
+        load(g_sb, g, 0, slice(0, 1), all_t)
+        load(dh_sb, dh, 0, slice(0, 1), all_t)
+        load(g_sb, g, 0, slice(1, 2), all_t)
+        load(g_sb, g, 0, slice(2, 3), all_t)
+        load(dh_sb, dh, 0, slice(1, 2), all_t)
+        load(g_sb, g, 0, slice(3, 4), all_t)
+        load(dh_sb, dh, 0, slice(2, 3), all_t)
+        load(dh_sb, dh, 0, slice(3, 4), all_t)
         for dst, src, a in ((u_sb, u, 0), (g_sb, g, 1), (u_sb, u, 1), (dh_sb, dh, 1)):
             load(dst, src, a, lo_j, all_t)
             load(dst, src, a, hi_j, all_t)
@@ -101,8 +101,9 @@ def tile_mix_glubwd_fm_none_kernel(tc, g, u, dh, wg_words, wg_scales, wu_words, 
                     in_=scales.bitcast(I32)[:, 4 * q:4 * q + 4, :].rearrange("a r n -> r a n"),
                 )
         nc.sync.dma_start(out=wg_sb[:].bitcast(I32), in_=wg_words.rearrange("a p n -> p a n").bitcast(I32))
+        load(u_sb, u, 2, all_j, lo_t)
         nc.sync.dma_start(out=wu_sb[:].bitcast(I32), in_=wu_words.rearrange("a p n i -> p a (n i)").bitcast(I32))
-        load(u_sb, u, 2, all_j, all_t)
+        load(u_sb, u, 2, all_j, hi_t)
 
         def sigmoid(a, js, ts):
             nc.scalar.activation(out=stage("sig", a)[:, js, ts], in_=g_sb[a][:, js, ts], func=ACT.Sigmoid)
@@ -160,15 +161,18 @@ def tile_mix_glubwd_fm_none_kernel(tc, g, u, dh, wg_words, wg_scales, wu_words, 
                 lhsT_scale=wg_plane[:, a, P * m:P * (m + 1)],
                 rhs=dg_codes[a][:, cols].bitcast(E5M2X4), rhs_scale=dg_scale[a][:, cols], start=start, stop=stop)
 
-        for js, ts in head:
-            sigmoid(0, js, ts)
-        for js, ts in head[:3]:
-            make_a(0, js, ts)
-            make_du(0, js, ts)
-        for js, ts in head[3:]:
-            make_a(0, js, ts)
-        for js, ts in head[3:]:
-            make_du(0, js, ts)
+        sigmoid(0, slice(0, 1), all_t)
+        sigmoid(0, slice(1, 2), all_t)
+        sigmoid(0, slice(2, 3), all_t)
+        sigmoid(0, slice(3, 4), all_t)
+        make_a(0, slice(0, 1), all_t)
+        make_du(0, slice(0, 1), all_t)
+        make_a(0, slice(1, 2), all_t)
+        make_du(0, slice(1, 2), all_t)
+        make_a(0, slice(2, 3), all_t)
+        make_a(0, slice(3, 4), all_t)
+        make_du(0, slice(2, 3), all_t)
+        make_du(0, slice(3, 4), all_t)
         silu_neg(0, slice(0, 1), all_t)
         silu_neg(0, slice(1, 2), all_t)
         silu_neg(0, hi_j, lo_t)
@@ -184,30 +188,30 @@ def tile_mix_glubwd_fm_none_kernel(tc, g, u, dh, wg_words, wg_scales, wu_words, 
         make_q(1, lo_j, all_t)
         quant_dg(0, all_t)
         make_q(1, hi_j, all_t)
+        early = slice(0, EARLY)
+        late = slice(EARLY, T)
+        late_a = slice(EARLY, EARLY + LATE // 2)
+        late_b = slice(EARLY + LATE // 2, T)
         sigmoid(1, lo_j, all_t)
         sigmoid(1, hi_j, all_t)
         round_du(0, all_t)
         sigmoid(2, lo_j, all_t)
         sigmoid(2, hi_j, all_t)
+        silu_neg(2, all_j, early)
+        silu_neg(2, all_j, late)
         make_a(1, lo_j, all_t)
         make_a(1, hi_j, all_t)
         make_du(1, lo_j, all_t)
         make_du(1, hi_j, all_t)
         round_du(1, all_t)
+        make_dg(1, all_t)
         quant_du(0, all_t)
         make_a(2, lo_j, all_t)
         make_a(2, hi_j, all_t)
         make_du(2, lo_j, all_t)
         make_du(2, hi_j, all_t)
-        quant_du(1, all_t)
-        make_dg(1, all_t)
-        early = slice(0, EARLY)
-        late = slice(EARLY, T)
-        late_a = slice(EARLY, EARLY + LATE // 2)
-        late_b = slice(EARLY + LATE // 2, T)
-        silu_neg(2, all_j, early)
-        silu_neg(2, all_j, late)
         round_du(2, all_t)
+        quant_du(1, all_t)
         make_q(2, all_j, early)
         quant_dg(1, all_t)
         make_dg(2, early)
@@ -222,13 +226,14 @@ def tile_mix_glubwd_fm_none_kernel(tc, g, u, dh, wg_words, wg_scales, wu_words, 
 
         for m in range(M_TILES):
             mm_dg(0, m, acc[m], all_t, True, False)
-        for a in range(2):
-            for m in range(M_TILES):
-                mm_du(a, m)
+        for m in range(M_TILES):
+            mm_du(0, m)
+        for m in range(M_TILES):
+            mm_du(1, m)
         for m in range(M_TILES):
             mm_dg(1, m, acc[m], all_t, False, False)
         for m in range(M_TILES):
-            mm_du(LAST, m)
+            mm_du(2, m)
         for m in range(M_TILES):
             mm_dg(LAST, m, acc[m], all_t, False, True)
             nc.scalar.copy(out=res[m][:, early], in_=acc[m][:, early])

@@ -1,6 +1,7 @@
 from contextlib import ExitStack
 
 import concourse.mybir as mybir
+from concourse.masks import make_identity
 
 H, D, T = 1536, 512, 512
 FLOPS = 2 * 2 * H * D * T
@@ -23,6 +24,7 @@ M_TILES = D // P
 LAST = PASSES - 1
 LATE = 256
 EARLY = T - LATE
+POOL_T = 192
 
 
 def tile_mix_glubwd_fm_none_kernel(tc, g, u, dh, wg_words, wg_scales, wu_words, wu_scales, out):
@@ -50,10 +52,7 @@ def tile_mix_glubwd_fm_none_kernel(tc, g, u, dh, wg_words, wg_scales, wu_words, 
         wu_sb = keep.tile([P, PASSES, 4 * D], U8, align_bytes=64)
         wg_plane = keep.tile([P, PASSES, D], U8, align_bytes=64)
         wu_plane = keep.tile([P, PASSES, D], U8, align_bytes=64)
-        warm = keep.tile([P, 8], F32, align_bytes=64)
-        warm_out = keep.tile([P, 8], F32, align_bytes=64)
-        acc = [psum.tile([P, T], F32, name="acc" + str(m)) for m in range(M_TILES)]
-        acc_late = [psum.tile([P, T], F32, name="acc_late" + str(m)) for m in range(M_TILES)]
+        ident = keep.tile([P, P], F32, align_bytes=64)
         part = [keep.tile([P, LATE], F32, name="part" + str(m), align_bytes=64) for m in range(M_TILES)]
         res = [keep.tile([P, T], F32, name="res" + str(m), align_bytes=64) for m in range(M_TILES)]
 
@@ -64,8 +63,7 @@ def tile_mix_glubwd_fm_none_kernel(tc, g, u, dh, wg_words, wg_scales, wu_words, 
                 scratch[(kind, a)] = work.tile([P, PACK, T], F32, name=kind, align_bytes=64)
             return scratch[(kind, a)]
 
-        nc.vector.memset(warm[:], 0.0)
-        nc.scalar.activation(out=warm_out[:], in_=warm[:], func=ACT.Sigmoid)
+        make_identity(nc, ident[:])
         nc.vector.memset(wg_plane[:].bitcast(U32), 0)
         nc.vector.memset(wu_plane[:].bitcast(U32), 0)
         nc.vector.memset(dg_codes[LAST][:, EARLY:T], 0)
@@ -74,6 +72,7 @@ def tile_mix_glubwd_fm_none_kernel(tc, g, u, dh, wg_words, wg_scales, wu_words, 
         all_t = slice(0, T)
         all_j = slice(0, PACK)
         lo_j, hi_j = slice(0, 2), slice(2, 4)
+        vec_t, pool_t = slice(0, T - POOL_T), slice(T - POOL_T, T)
         lo_t, hi_t = slice(0, T // 2), slice(T // 2, T)
 
         def load(dst, src, a, js, ts):
@@ -91,7 +90,8 @@ def tile_mix_glubwd_fm_none_kernel(tc, g, u, dh, wg_words, wg_scales, wu_words, 
         for dst, src, a in ((u_sb, u, 0), (g_sb, g, 1), (u_sb, u, 1), (dh_sb, dh, 1)):
             load(dst, src, a, lo_j, all_t)
             load(dst, src, a, hi_j, all_t)
-        load(g_sb, g, 2, all_j, all_t)
+        load(g_sb, g, 2, lo_j, all_t)
+        load(g_sb, g, 2, hi_j, all_t)
         load(dh_sb, dh, 2, lo_j, all_t)
         load(dh_sb, dh, 2, hi_j, all_t)
         for plane, scales in ((wg_plane, wg_scales), (wu_plane, wu_scales)):
@@ -116,6 +116,23 @@ def tile_mix_glubwd_fm_none_kernel(tc, g, u, dh, wg_words, wg_scales, wu_words, 
                 out=neg_a[a][:, js, ts], in0=stage("sig", a)[:, js, ts], scalar=-1.0, in1=dh_sb[a][:, js, ts],
                 op0=ALU.mult, op1=ALU.mult)
 
+        def banks(name):
+            return [psum.tile([P, T], F32, name=name + str(n)) for n in range(PACK)]
+
+        def turn(bank, src):
+            for tb in range(T // P):
+                nc.tensor.transpose(bank[:, P * tb:P * (tb + 1)], src[:, P * tb:P * (tb + 1)], ident[:])
+
+        def sigmoid_turned(a, j, bank):
+            nc.scalar.activation(out=stage("sig", a)[:, j, :], in_=bank[:], func=ACT.Sigmoid)
+
+        def make_a_psum(a, j, bank):
+            nc.vector.scalar_tensor_tensor(
+                out=neg_a[a][:, j, :], in0=bank[:], scalar=-1.0, in1=dh_sb[a][:, j, :], op0=ALU.mult, op1=ALU.mult)
+
+        def make_du_pool(a, dst):
+            nc.gpsimd.tensor_tensor(out=dst[:, :, pool_t], in0=neg_a[a][:, :, pool_t], in1=g_sb[a][:, :, pool_t], op=ALU.mult)
+
         def make_du(a, js, ts):
             nc.vector.tensor_tensor(
                 out=stage("neg_du", a)[:, js, ts], in0=neg_a[a][:, js, ts], in1=g_sb[a][:, js, ts], op=ALU.mult)
@@ -135,8 +152,8 @@ def tile_mix_glubwd_fm_none_kernel(tc, g, u, dh, wg_words, wg_scales, wu_words, 
             nc.vector.tensor_tensor(
                 out=words_view(dg_bf[a], ts), in0=rows_view(neg_a[a], ts), in1=rows_view(stage("neg_q", a), ts), op=ALU.mult)
 
-        def round_du(a, ts):
-            nc.scalar.activation(out=words_view(du_bf[a], ts), in_=rows_view(stage("neg_du", a), ts), func=ACT.Copy, scale=-1.0)
+        def round_du(a, ts, src):
+            nc.scalar.activation(out=words_view(du_bf[a], ts), in_=rows_view(src, ts), func=ACT.Copy, scale=-1.0)
 
         def quantize(vals, codes, scale, ts, shift):
             cols = slice(ts.start + shift, ts.stop + shift)
@@ -194,26 +211,33 @@ def tile_mix_glubwd_fm_none_kernel(tc, g, u, dh, wg_words, wg_scales, wu_words, 
         late_b = slice(EARLY + LATE // 2, T)
         sigmoid(1, lo_j, all_t)
         sigmoid(1, hi_j, all_t)
-        round_du(0, all_t)
-        sigmoid(2, lo_j, all_t)
-        sigmoid(2, hi_j, all_t)
-        silu_neg(2, all_j, early)
-        silu_neg(2, all_j, late)
         make_a(1, lo_j, all_t)
         make_a(1, hi_j, all_t)
-        make_du(1, lo_j, all_t)
-        make_du(1, hi_j, all_t)
-        round_du(1, all_t)
+        round_du(0, all_t, stage("neg_du", 0))
+        turned = banks("upper")
+        for j in range(PACK):
+            turn(turned[j], g_sb[2][:, j, :])
+        back = banks("lower")
+        for j in range(PACK):
+            sigmoid_turned(2, j, turned[j])
+            turn(back[j], stage("sig", 2)[:, j, :])
+        make_du(1, lo_j, vec_t)
+        make_du(1, hi_j, vec_t)
+        silu_neg(2, all_j, early)
+        silu_neg(2, all_j, late)
         make_dg(1, all_t)
-        quant_du(0, all_t)
-        make_a(2, lo_j, all_t)
-        make_a(2, hi_j, all_t)
+        make_du_pool(1, stage("neg_q", 1))
+        for j in range(PACK):
+            make_a_psum(2, j, back[j])
+        round_du(1, vec_t, stage("neg_du", 1))
+        round_du(1, pool_t, stage("neg_q", 1))
+        quant_dg(1, all_t)
         make_du(2, lo_j, all_t)
         make_du(2, hi_j, all_t)
-        round_du(2, all_t)
-        quant_du(1, all_t)
+        round_du(2, all_t, stage("neg_du", 2))
+        quant_du(0, all_t)
         make_q(2, all_j, early)
-        quant_dg(1, all_t)
+        quant_du(1, all_t)
         make_dg(2, early)
         quant_du(2, all_t)
         make_q(2, all_j, late_a)
@@ -223,17 +247,16 @@ def tile_mix_glubwd_fm_none_kernel(tc, g, u, dh, wg_words, wg_scales, wu_words, 
         make_dg(2, late_b)
         quant_dg(2, late_a, LATE)
         quant_dg(2, late_b, LATE)
+        acc = banks("lower")
+        acc_late = banks("upper")
 
         for m in range(M_TILES):
             mm_dg(0, m, acc[m], all_t, True, False)
         for m in range(M_TILES):
-            mm_du(0, m)
-        for m in range(M_TILES):
-            mm_du(1, m)
-        for m in range(M_TILES):
             mm_dg(1, m, acc[m], all_t, False, False)
-        for m in range(M_TILES):
-            mm_du(2, m)
+        for a in range(PASSES):
+            for m in range(M_TILES):
+                mm_du(a, m)
         for m in range(M_TILES):
             mm_dg(LAST, m, acc[m], all_t, False, True)
             nc.scalar.copy(out=res[m][:, early], in_=acc[m][:, early])

from contextlib import ExitStack

import concourse.mybir as mybir
from concourse.masks import make_identity

H, D, T = 1536, 512, 512
FLOPS = 2 * 2 * H * D * T

F32 = mybir.dt.float32
BF16 = mybir.dt.bfloat16
I32 = mybir.dt.int32
U32 = mybir.dt.uint32
U8 = mybir.dt.uint8
E5M2X4 = mybir.dt.float8_e5m2_x4
E4M3X4 = mybir.dt.float8_e4m3fn_x4
E2M1X4 = mybir.dt.float4_e2m1fn_x4
ACT = mybir.ActivationFunctionType
ALU = mybir.AluOpType

P = 128
PACK = 4
PASSES = H // (P * PACK)
M_TILES = D // P
LAST = PASSES - 1
LATE = 256
EARLY = T - LATE
POOL_T = 192


def tile_mix_glubwd_fm_none_kernel(tc, g, u, dh, wg_words, wg_scales, wu_words, wu_scales, out):
    nc = tc.nc
    with ExitStack() as ctx:
        keep = ctx.enter_context(tc.tile_pool(name="keep", bufs=1))
        work = ctx.enter_context(tc.tile_pool(name="work", bufs=2))
        psum = ctx.enter_context(tc.psum_pool(name="psum", bufs=1))
        ctx.enter_context(tc.manual_schedule())

        def per_pass(name, shape, dtype):
            return [keep.tile(shape, dtype, name=name + str(a), align_bytes=64) for a in range(PASSES)]

        g_sb = per_pass("g_sb", [P, PACK, T], F32)
        u_sb = per_pass("u_sb", [P, PACK, T], F32)
        dh_sb = per_pass("dh_sb", [P, PACK, T], F32)
        neg_a = per_pass("neg_a", [P, PACK, T], F32)
        du_bf = per_pass("du_bf", [P, T, PACK], BF16)
        dg_bf = per_pass("dg_bf", [P, T, PACK], BF16)
        du_codes = per_pass("du_codes", [P, T], U32)
        dg_codes = per_pass("dg_codes", [P, T + LATE], U32)
        du_scale = per_pass("du_scale", [P, T], U8)
        dg_scale = per_pass("dg_scale", [P, T + LATE], U8)
        wg_sb = keep.tile([P, PASSES, 2 * D], U8, align_bytes=64)
        wu_sb = keep.tile([P, PASSES, 4 * D], U8, align_bytes=64)
        wg_plane = keep.tile([P, PASSES, D], U8, align_bytes=64)
        wu_plane = keep.tile([P, PASSES, D], U8, align_bytes=64)
        ident = keep.tile([P, P], F32, align_bytes=64)
        part = [keep.tile([P, LATE], F32, name="part" + str(m), align_bytes=64) for m in range(M_TILES)]
        res = [keep.tile([P, T], F32, name="res" + str(m), align_bytes=64) for m in range(M_TILES)]

        scratch = {}

        def stage(kind, a):
            if (kind, a) not in scratch:
                scratch[(kind, a)] = work.tile([P, PACK, T], F32, name=kind, align_bytes=64)
            return scratch[(kind, a)]

        make_identity(nc, ident[:])
        nc.vector.memset(wg_plane[:].bitcast(U32), 0)
        nc.vector.memset(wu_plane[:].bitcast(U32), 0)
        nc.vector.memset(dg_codes[LAST][:, EARLY:T], 0)
        nc.vector.memset(dg_scale[LAST][:, EARLY:T].bitcast(U32), 0)

        all_t = slice(0, T)
        all_j = slice(0, PACK)
        lo_j, hi_j = slice(0, 2), slice(2, 4)
        vec_t, pool_t = slice(0, T - POOL_T), slice(T - POOL_T, T)
        lo_t, hi_t = slice(0, T // 2), slice(T // 2, T)

        def load(dst, src, a, js, ts):
            rows = src[a * P * PACK:(a + 1) * P * PACK, :].rearrange("(p j) t -> p j t", j=PACK)
            nc.sync.dma_start(out=dst[a][:, js, ts], in_=rows[:, js, ts])

        load(g_sb, g, 0, slice(0, 1), all_t)
        load(dh_sb, dh, 0, slice(0, 1), all_t)
        load(g_sb, g, 0, slice(1, 2), all_t)
        load(g_sb, g, 0, slice(2, 3), all_t)
        load(dh_sb, dh, 0, slice(1, 2), all_t)
        load(g_sb, g, 0, slice(3, 4), all_t)
        load(dh_sb, dh, 0, slice(2, 3), all_t)
        load(dh_sb, dh, 0, slice(3, 4), all_t)
        for dst, src, a in ((u_sb, u, 0), (g_sb, g, 1), (u_sb, u, 1), (dh_sb, dh, 1)):
            load(dst, src, a, lo_j, all_t)
            load(dst, src, a, hi_j, all_t)
        load(g_sb, g, 2, lo_j, all_t)
        load(g_sb, g, 2, hi_j, all_t)
        load(dh_sb, dh, 2, lo_j, all_t)
        load(dh_sb, dh, 2, hi_j, all_t)
        for plane, scales in ((wg_plane, wg_scales), (wu_plane, wu_scales)):
            for q in range(4):
                nc.sync.dma_start(
                    out=plane[32 * q:32 * q + 4, :, :].bitcast(I32),
                    in_=scales.bitcast(I32)[:, 4 * q:4 * q + 4, :].rearrange("a r n -> r a n"),
                )
        nc.sync.dma_start(out=wg_sb[:].bitcast(I32), in_=wg_words.rearrange("a p n -> p a n").bitcast(I32))
        load(u_sb, u, 2, all_j, lo_t)
        nc.sync.dma_start(out=wu_sb[:].bitcast(I32), in_=wu_words.rearrange("a p n i -> p a (n i)").bitcast(I32))
        load(u_sb, u, 2, all_j, hi_t)

        def sigmoid(a, js, ts):
            nc.scalar.activation(out=stage("sig", a)[:, js, ts], in_=g_sb[a][:, js, ts], func=ACT.Sigmoid)

        def silu_neg(a, js, ts):
            nc.scalar.activation(out=stage("siln", a)[:, js, ts], in_=g_sb[a][:, js, ts], func=ACT.Silu, scale=-1.0)

        def make_a(a, js, ts):
            nc.vector.scalar_tensor_tensor(
                out=neg_a[a][:, js, ts], in0=stage("sig", a)[:, js, ts], scalar=-1.0, in1=dh_sb[a][:, js, ts],
                op0=ALU.mult, op1=ALU.mult)

        def banks(name):
            return [psum.tile([P, T], F32, name=name + str(n)) for n in range(PACK)]

        def turn(bank, src):
            for tb in range(T // P):
                nc.tensor.transpose(bank[:, P * tb:P * (tb + 1)], src[:, P * tb:P * (tb + 1)], ident[:])

        def sigmoid_turned(a, j, bank):
            nc.scalar.activation(out=stage("sig", a)[:, j, :], in_=bank[:], func=ACT.Sigmoid)

        def make_a_psum(a, j, bank):
            nc.vector.scalar_tensor_tensor(
                out=neg_a[a][:, j, :], in0=bank[:], scalar=-1.0, in1=dh_sb[a][:, j, :], op0=ALU.mult, op1=ALU.mult)

        def make_du_pool(a, dst):
            nc.gpsimd.tensor_tensor(out=dst[:, :, pool_t], in0=neg_a[a][:, :, pool_t], in1=g_sb[a][:, :, pool_t], op=ALU.mult)

        def make_du(a, js, ts):
            nc.vector.tensor_tensor(
                out=stage("neg_du", a)[:, js, ts], in0=neg_a[a][:, js, ts], in1=g_sb[a][:, js, ts], op=ALU.mult)

        def make_q(a, js, ts):
            nc.vector.scalar_tensor_tensor(
                out=stage("neg_q", a)[:, js, ts], in0=stage("siln", a)[:, js, ts], scalar=-1.0, in1=u_sb[a][:, js, ts],
                op0=ALU.add, op1=ALU.mult)

        def rows_view(tile, ts):
            return tile[:, :, ts].rearrange("p j (c i) -> p c j i", i=4)

        def words_view(tile, ts):
            return tile[:, ts, :].rearrange("p (c i) j -> p c j i", i=4)

        def make_dg(a, ts):
            nc.vector.tensor_tensor(
                out=words_view(dg_bf[a], ts), in0=rows_view(neg_a[a], ts), in1=rows_view(stage("neg_q", a), ts), op=ALU.mult)

        def round_du(a, ts, src):
            nc.scalar.activation(out=words_view(du_bf[a], ts), in_=rows_view(src, ts), func=ACT.Copy, scale=-1.0)

        def quantize(vals, codes, scale, ts, shift):
            cols = slice(ts.start + shift, ts.stop + shift)
            nc.vector.quantize_mx(
                out=codes[:, cols].bitcast(E5M2X4), scales=scale[:, cols], in_=vals[:, ts, :].rearrange("p t j -> p (t j)"))

        def quant_du(a, ts):
            quantize(du_bf[a], du_codes[a], du_scale[a], ts, 0)

        def quant_dg(a, ts, shift=0):
            quantize(dg_bf[a], dg_codes[a], dg_scale[a], ts, shift)

        def mm_du(a, m):
            nc.tensor.matmul_mx(
                out=acc[m][:], lhsT=wu_sb[:, a, 4 * P * m:4 * P * (m + 1)].bitcast(E4M3X4),
                lhsT_scale=wu_plane[:, a, P * m:P * (m + 1)],
                rhs=du_codes[a][:].bitcast(E5M2X4), rhs_scale=du_scale[a][:], start=False, stop=False)

        def mm_dg(a, m, bank, cols, start, stop):
            nc.tensor.matmul_mx(
                out=bank[:], lhsT=wg_sb[:, a, 2 * P * m:2 * P * (m + 1)].bitcast(E2M1X4),
                lhsT_scale=wg_plane[:, a, P * m:P * (m + 1)],
                rhs=dg_codes[a][:, cols].bitcast(E5M2X4), rhs_scale=dg_scale[a][:, cols], start=start, stop=stop)

        sigmoid(0, slice(0, 1), all_t)
        sigmoid(0, slice(1, 2), all_t)
        sigmoid(0, slice(2, 3), all_t)
        sigmoid(0, slice(3, 4), all_t)
        make_a(0, slice(0, 1), all_t)
        make_du(0, slice(0, 1), all_t)
        make_a(0, slice(1, 2), all_t)
        make_du(0, slice(1, 2), all_t)
        make_a(0, slice(2, 3), all_t)
        make_a(0, slice(3, 4), all_t)
        make_du(0, slice(2, 3), all_t)
        make_du(0, slice(3, 4), all_t)
        silu_neg(0, slice(0, 1), all_t)
        silu_neg(0, slice(1, 2), all_t)
        silu_neg(0, hi_j, lo_t)
        silu_neg(0, hi_j, hi_t)
        silu_neg(1, lo_j, all_t)
        silu_neg(1, hi_j, all_t)
        make_q(0, slice(0, 1), all_t)
        make_q(0, slice(1, 2), all_t)
        make_q(0, hi_j, lo_t)
        make_q(0, hi_j, hi_t)
        make_dg(0, lo_t)
        make_dg(0, hi_t)
        make_q(1, lo_j, all_t)
        quant_dg(0, all_t)
        make_q(1, hi_j, all_t)
        early = slice(0, EARLY)
        late = slice(EARLY, T)
        late_a = slice(EARLY, EARLY + LATE // 2)
        late_b = slice(EARLY + LATE // 2, T)
        sigmoid(1, lo_j, all_t)
        sigmoid(1, hi_j, all_t)
        make_a(1, lo_j, all_t)
        make_a(1, hi_j, all_t)
        round_du(0, all_t, stage("neg_du", 0))
        turned = banks("upper")
        for j in range(PACK):
            turn(turned[j], g_sb[2][:, j, :])
        back = banks("lower")
        for j in range(PACK):
            sigmoid_turned(2, j, turned[j])
            turn(back[j], stage("sig", 2)[:, j, :])
        make_du(1, lo_j, vec_t)
        make_du(1, hi_j, vec_t)
        silu_neg(2, all_j, early)
        silu_neg(2, all_j, late)
        make_dg(1, all_t)
        make_du_pool(1, stage("neg_q", 1))
        for j in range(PACK):
            make_a_psum(2, j, back[j])
        round_du(1, vec_t, stage("neg_du", 1))
        round_du(1, pool_t, stage("neg_q", 1))
        quant_dg(1, all_t)
        make_du(2, lo_j, all_t)
        make_du(2, hi_j, all_t)
        round_du(2, all_t, stage("neg_du", 2))
        quant_du(0, all_t)
        make_q(2, all_j, early)
        quant_du(1, all_t)
        make_dg(2, early)
        quant_du(2, all_t)
        make_q(2, all_j, late_a)
        quant_dg(2, early)
        make_q(2, all_j, late_b)
        make_dg(2, late_a)
        make_dg(2, late_b)
        quant_dg(2, late_a, LATE)
        quant_dg(2, late_b, LATE)
        acc = banks("lower")
        acc_late = banks("upper")

        for m in range(M_TILES):
            mm_dg(0, m, acc[m], all_t, True, False)
        for m in range(M_TILES):
            mm_dg(1, m, acc[m], all_t, False, False)
        for a in range(PASSES):
            for m in range(M_TILES):
                mm_du(a, m)
        for m in range(M_TILES):
            mm_dg(LAST, m, acc[m], all_t, False, True)
            nc.scalar.copy(out=res[m][:, early], in_=acc[m][:, early])
            nc.sync.dma_start(out=out[P * m:P * (m + 1), early], in_=res[m][:, early])
        for m in range(M_TILES):
            nc.scalar.copy(out=part[m][:], in_=acc[m][:, late])
        for m in range(M_TILES):
            mm_dg(LAST, m, acc_late[m], slice(LATE, T + LATE), True, True)
            nc.vector.tensor_tensor(out=res[m][:, late], in0=acc_late[m][:, late], in1=part[m][:], op=ALU.add)
            nc.sync.dma_start(out=out[P * m:P * (m + 1), late], in_=res[m][:, late])
